import numpy as np
import ml_dtypes


def mxq(x, axis, fmt="e4m3"):
    dtype, down = {"e4m3": (ml_dtypes.float8_e4m3fn, 7), "e5m2": (ml_dtypes.float8_e5m2, 14)}[fmt]
    v = np.moveaxis(np.asarray(x, np.float32).astype(ml_dtypes.bfloat16).astype(np.float64), axis, -1)
    blocks = v.reshape(v.shape[:-1] + (-1, 32))
    amax = np.abs(blocks).max(-1, keepdims=True)
    byte = np.maximum(np.where(amax > 0, np.frexp(amax)[1] - 1 + 127, 0) - down, 1)
    scale = np.exp2(byte - 127.0)
    codes = (blocks / scale).astype(np.float32).astype(dtype).astype(np.float64)
    return np.moveaxis((codes * scale).reshape(v.shape), -1, axis)


WIDE = False


def mx_kscale(k):
    if not WIDE:
        return np.ones(k)
    levels = np.array([10, -10, 5, -5, 0])
    if k % 512:
        return np.exp2(np.random.permutation(np.resize(levels, k // 32))).repeat(32)
    a = np.empty((k // 512, 16))
    for p in range(k // 512):
        a[p, :8] = np.random.permutation(np.resize(levels, 8))
        for g in range(8):
            far = levels[np.abs(levels - a[p, g]) >= 10]
            a[p, g + 8] = far[np.random.randint(len(far))]
    return np.exp2(a.ravel()).repeat(32)


BF16 = ml_dtypes.bfloat16


def bf(x):
    return np.asarray(x, np.float32).astype(BF16)


def f64(x):
    return np.asarray(x).astype(np.float64)


E2M1 = np.array([0.0, 0.5, 1.0, 1.5, 2.0, 3.0, 4.0, 6.0, -0.0, -0.5, -1.0, -1.5, -2.0, -3.0, -4.0, -6.0])


def pack_weight(w, fmt):
    k, n = w.shape
    w = f64(bf(w)).reshape(k // 32, 32, n)
    amax = np.abs(w).max(1)
    if fmt == "e4m3":
        byte = np.frexp(amax)[1] - 1 + 127 - 7
    else:
        mant, ex = np.frexp(amax / 6.0)
        byte = np.where(mant > 0.5, ex, ex - 1) + 127
    byte = np.clip(np.where(amax > 0, byte, 1), 1, 254)
    scaled = (w * np.exp2(127.0 - byte)[:, None, :]).reshape(k, n).astype(np.float32)
    by_word = np.ascontiguousarray(scaled.reshape(k // 512, 128, 4, n).transpose(0, 1, 3, 2))
    if fmt == "e4m3":
        words = by_word.astype(ml_dtypes.float8_e4m3fn).view(np.uint8)
    else:
        c = by_word.astype(ml_dtypes.float4_e2m1fn).view(np.uint8) & 0xF
        words = c[..., 0::2] | (c[..., 1::2] << 4)
    return np.ascontiguousarray(words), np.ascontiguousarray(byte.astype(np.uint8).reshape(k // 512, 16, n))


def unpack_weight(words, scales, fmt):
    g, p, n, _ = words.shape
    if fmt == "e4m3":
        vals = np.ascontiguousarray(words).view(ml_dtypes.float8_e4m3fn).astype(np.float64)
    else:
        nib = np.empty((g, p, n, 4), np.uint8)
        nib[..., 0::2] = words & 0xF
        nib[..., 1::2] = words >> 4
        vals = E2M1[nib]
    vals = vals * np.repeat(np.exp2(scales.astype(np.float64) - 127.0), 8, axis=1)[..., None]
    return vals.transpose(0, 1, 3, 2).reshape(g * 512, n)
def pack4(w):
    words, scales = pack_weight(w, "e2m1")
    return words.reshape(words.shape[0], 128, -1), scales


def unpack4(words, scales):
    return unpack_weight(words.reshape(words.shape[0], 128, -1, 2), scales, "e2m1")


C, J, X, R = 1024, 1536, 1536, 1024


def setup_inputs():
    s, t = mx_kscale(J), mx_kscale(C)
    inverse = np.random.standard_normal((C, J)) / np.sqrt(J) * s * t[:, None]
    images = np.random.standard_normal((J, X)) / s[:, None]
    lights = np.random.standard_normal((C, R)) / np.sqrt(C) / t[:, None]
    lights_words, lights_scales = pack4(lights)
    return {"inverse": bf(inverse),
            "images": bf(images),
            "mean_coef": bf(0.3 * np.random.standard_normal(C) * t),
            "albedo": bf(np.random.uniform(0.5, 1.5, X)),
            "lights_words": lights_words,
            "lights_scales": lights_scales}


def reference(inverse, images, mean_coef, albedo, lights_words, lights_scales):
    scaled = mxq(f64(inverse), 1, "e4m3") @ mxq(f64(images), 0, "e4m3")
    normals = (scaled + f64(mean_coef)[:, None]) / f64(albedo)[None, :]
    shading = mxq(normals, 0, "e4m3").T @ unpack4(lights_words, lights_scales)
    return np.maximum(shading, 0.0)

@@ -1,0 +1,272 @@
+from contextlib import ExitStack
+
+import concourse.mybir as mybir
+from concourse.masks import make_identity
+
+C, J, X, R = 1024, 1536, 1536, 1024
+FLOPS = 2 * C * J * X + 2 * X * C * R
+
+F32 = mybir.dt.float32
+BF16 = mybir.dt.bfloat16
+I32 = mybir.dt.int32
+U32 = mybir.dt.uint32
+U8 = mybir.dt.uint8
+E4M3 = mybir.dt.float8_e4m3fn_x4
+E2M1 = mybir.dt.float4_e2m1fn_x4
+ALU = mybir.AluOpType
+ACT = mybir.ActivationFunctionType
+P = 128
+
+
+def tile_photometric_stereo_shading_s13_kernel(
+    tc, inverse, images, mean_coef, albedo, lights_words, lights_scales, out
+):
+    nc = tc.nc
+    with ExitStack() as ctx:
+        keep = ctx.enter_context(tc.tile_pool(name="keep", bufs=1))
+        psum = ctx.enter_context(tc.psum_pool(name="psum", bufs=1))
+        ctx.enter_context(tc.manual_schedule())
+
+        ident = keep.tile([P, P], F32, name="ident")
+        make_identity(nc, ident[:])
+        alb = keep.tile([P, 3, 4], BF16, name="alb")
+        ralb = keep.tile([P, 12], F32, name="ralb")
+        mean = keep.tile([P, 2, 4], BF16, name="mean")
+        w_words = keep.tile([P, 2, 2 * R], U8, name="w_words", align_bytes=64)
+        w_scales = keep.tile([P, 2, R], U8, name="w_scales", align_bytes=64)
+        T = {}
+        banks = {}
+
+        def new(kind, key, shape, dtype, bufs=None):
+            name = "%s_%d_%d" % (kind, key[0], key[1])
+            if bufs is None:
+                T[kind, key] = keep.tile(shape, dtype, name=name, align_bytes=64)
+            else:
+                T[kind, key] = keep.tile(shape, dtype, name=name, tag=kind, bufs=bufs, align_bytes=64)
+            return T[kind, key]
+
+        def bank(b):
+            banks[b] = psum.tile([P, 512], F32, name="bank%d" % b, tag="bank%d" % b)
+            return banks[b]
+
+        def memset():
+            nc.vector.memset(w_scales[:].rearrange("p g n -> p (g n)").bitcast(I32), 0)
+
+        def load_small(n):
+            if n == "alb":
+                nc.sync.dma_start(out=alb[:], in_=albedo.rearrange("(j p i) -> p j i", p=P, i=4))
+            elif n == "mean":
+                nc.sync.dma_start(out=mean[:], in_=mean_coef.rearrange("(c p t) -> p c t", p=P, t=4))
+            else:
+                for q in range(4):
+                    nc.sync.dma_start(
+                        out=w_scales[32 * q : 32 * q + 4, :, :].bitcast(I32),
+                        in_=lights_scales[:, 4 * q : 4 * q + 4, :].rearrange("g r n -> r g n").bitcast(I32),
+                    )
+
+        def load_a(c, g):
+            raw = new("a_raw", (c, g), [P, 4, 512], BF16)
+            src = inverse[512 * c : 512 * (c + 1), 512 * g : 512 * (g + 1)]
+            nc.sync.dma_start(out=raw[:], in_=src.rearrange("(m t) k -> m t k", t=4))
+
+        def load_b(j, g):
+            raw = new("b_raw", (j, g), [P, 4, 512], BF16)
+            src = images[512 * g : 512 * (g + 1), 512 * j : 512 * (j + 1)]
+            nc.sync.dma_start(out=raw[:], in_=src.rearrange("(p t) x -> p t x", t=4))
+
+        def load_w():
+            nc.sync.dma_start(out=w_words[:].bitcast(I32), in_=lights_words.rearrange("g p b -> p g b").bitcast(I32))
+
+        def recip():
+            nc.vector.reciprocal(out=ralb[:], in_=alb[:].rearrange("p j i -> p (j i)"))
+
+        def spread(j, b):
+            acc = bank(b)
+            for i in range(4):
+                col = ralb[:, 4 * j + i : 4 * j + i + 1].to_broadcast([P, P])
+                nc.tensor.transpose(acc[:, P * i : P * (i + 1)], col, ident[:])
+
+        def copy_r(j, b):
+            rinv = new("rinv", (j, 0), [P, 512], F32)
+            nc.scalar.activation(
+                out=rinv[:].rearrange("p (n i) -> p n i", i=4),
+                in_=banks[b][:].rearrange("p (i n) -> p n i", i=4),
+                func=ACT.Copy,
+            )
+
+        def transpose_a(c, g, h, b):
+            acc = bank(b)
+            for t in range(2):
+                words = T["a_raw", (c, g)][:, 2 * h + t, :].bitcast(F32)
+                for u in range(2):
+                    nc.tensor.transpose(acc[:, P * (2 * t + u) : P * (2 * t + u + 1)], words[:, u:256:2], ident[:])
+
+        def copy_a(c, g, h, b):
+            if h == 0:
+                new("a_grp", (c, g), [P, 2048], BF16, bufs=3)
+            dst = T["a_grp", (c, g)][:].bitcast(F32)[:, 512 * h : 512 * (h + 1)]
+            nc.scalar.copy(
+                out=dst.rearrange("p (t m u) -> p t m u", t=2, u=2),
+                in_=banks[b][:].rearrange("p (t u m) -> p t m u", t=2, u=2),
+            )
+
+        def quant(kind, key, part):
+            if part != 1:
+                new(kind + "_codes", key, [P, 512], U32)
+                new(kind + "_scales", key, [P, 512], U8)
+            lo, hi = (0, 512) if part == "all" else (256 * part, 256 * part + 256)
+            nc.vector.quantize_mx(
+                out=T[kind + "_codes", key][:, lo:hi].bitcast(E4M3),
+                scales=T[kind + "_scales", key][:, lo:hi],
+                in_=T[kind + "_grp", key][:, 4 * lo : 4 * hi],
+            )
+
+        def weave(kind, key, e, part, bufs):
+            if part != 1:
+                new(kind + "_grp", key, [P, 2048], BF16, bufs=bufs)
+            lo, hi = (0, 512) if part == "all" else (256 * part, 256 * part + 256)
+            dst = T[kind + "_grp", key][:, 4 * lo : 4 * hi].rearrange("p (c i t) -> p c t i", i=4, t=4)
+            src = T[kind + "_raw", key][:, :, lo:hi].rearrange("p t (c i) -> p c t i", i=4)
+            if e == "V":
+                nc.vector.tensor_copy(out=dst, in_=src)
+            else:
+                nc.scalar.copy(out=dst, in_=src)
+
+        def quant_a(c, g):
+            quant("a", (c, g), "all")
+
+        def quant_b(j, g):
+            quant("b", (j, g), "all")
+
+        def quant_n(j, c, part="all"):
+            quant("n", (j, c), part)
+
+        def weave_b(j, g, e="V", part="all"):
+            weave("b", (j, g), e, part, 4)
+
+        def weave_n(j, c, e="S", part="all"):
+            weave("n", (j, c), e, part, 3)
+
+        def mm1(j, c, t, g, b):
+            if g == 0:
+                bank(b)
+            cols = slice(P * t, P * (t + 1))
+            nc.tensor.matmul_mx(
+                out=banks[b][:],
+                lhsT=T["a_codes", (c, g)][:, cols].bitcast(E4M3),
+                lhsT_scale=T["a_scales", (c, g)][:, cols],
+                rhs=T["b_codes", (j, g)][:].bitcast(E4M3),
+                rhs_scale=T["b_scales", (j, g)][:],
+                start=(g == 0),
+                stop=(g == 2),
+            )
+
+        def normals(j, c, t, b):
+            if t == 0:
+                new("n_raw", (j, c), [P, 4, 512], BF16, bufs=4)
+            nc.vector.scalar_tensor_tensor(
+                out=T["n_raw", (j, c)][:, t, :],
+                in0=banks[b][:],
+                scalar=mean[:, c, t : t + 1],
+                in1=T["rinv", (j, 0)][:],
+                op0=ALU.add,
+                op1=ALU.mult,
+            )
+
+        def mm2(x, h, c, b):
+            if c == 0:
+                bank(b)
+            cols = slice(P * (x % 4), P * (x % 4 + 1))
+            nc.tensor.matmul_mx(
+                out=banks[b][:],
+                lhsT=T["n_codes", (x // 4, c)][:, cols].bitcast(E4M3),
+                lhsT_scale=T["n_scales", (x // 4, c)][:, cols],
+                rhs=w_words[:, c, 1024 * h : 1024 * (h + 1)].bitcast(E2M1),
+                rhs_scale=w_scales[:, c, 512 * h : 512 * (h + 1)],
+                start=(c == 0),
+                stop=(c == 1),
+            )
+
+        def shade(x, h, b, e="S"):
+            if h == 0:
+                new("shading", (x, 0), [P, R], F32, bufs=8)
+            dst = T["shading", (x, 0)][:, 512 * h : 512 * (h + 1)]
+            if e == "V":
+                nc.vector.tensor_scalar_max(out=dst, in0=banks[b][:], scalar1=0.0)
+            else:
+                nc.scalar.activation(out=dst, in_=banks[b][:], func=ACT.Relu)
+
+        def store(x, h="all"):
+            lo, hi = (0, R) if h == "all" else (512 * h, 512 * h + 512)
+            nc.sync.dma_start(out=out[P * x : P * (x + 1), lo:hi], in_=T["shading", (x, 0)][:, lo:hi])
+
+
+        memset()
+        load_small('alb')
+        for g in range(3): load_a(0,g); load_b(0,g)
+        load_small('mean')
+        load_a(1,0); load_b(1,0); load_a(1,1); load_b(1,1); load_a(1,2); load_b(1,2)
+        load_b(2,0); load_w(); load_small('ws')
+        load_b(2,1); load_b(2,2)
+        recip()
+        def prep_a(s):
+            for h in range(2): transpose_a(s//3,s%3,h,6+h)
+            for h in range(2): copy_a(s//3,s%3,h,6+h)
+        def wb(j,g): weave_b(j,g,'V',0); weave_b(j,g,'S',1)
+        B0=[0,1,2,3]; B1=[4,5,0,1]; B2=[2,3,6,7]
+        spread(0,0); copy_r(0,0); prep_a(0); spread(1,4); spread(2,5)
+        weave_b(0,0,'V')
+        copy_r(1,4)
+        prep_a(1)
+        quant_a(0,0); quant_b(0,0)
+        for t in range(4): mm1(0,0,t,0,B0[t])
+        copy_r(2,5)
+        weave_b(0,1,'V'); quant_a(0,1); quant_b(0,1)
+        prep_a(2)
+        for t in range(4): mm1(0,0,t,1,B0[t])
+        weave_b(0,2,'V'); quant_b(0,2); quant_a(0,2)
+        wb(1,0)
+        prep_a(3)
+        for t in range(4): mm1(0,0,t,2,B0[t])
+        quant_b(1,0); quant_a(1,0);
+        prep_a(4)
+        normals(0,0,0,0); normals(0,0,1,1)
+        for t in range(4): mm1(0,1,t,0,B1[t])
+        wb(1,1); quant_a(1,1); normals(0,0,2,2); quant_b(1,1); normals(0,0,3,3)
+        prep_a(5)
+        for t in range(4): mm1(0,1,t,1,B1[t])
+        quant_a(1,2); wb(1,2);
+        for t in range(4): mm1(0,1,t,2,B1[t])
+        weave_n(0,0,'S'); quant_b(1,2)
+        normals(0,1,0,4); normals(0,1,1,5); normals(0,1,2,0); normals(0,1,3,1)
+        for t in range(4):
+            for g in range(3): mm1(1,0,t,g,B2[t])
+        weave_b(2,0,'S'); quant_n(0,0)
+        weave_n(0,1,'V');
+        normals(1,0,0,2); quant_n(0,1); normals(1,0,1,3); quant_b(2,0); normals(1,0,2,6); normals(1,0,3,7)
+        weave_b(2,1,'S'); wb(2,2)
+        u=[0]
+        def s2(n,e='S'):
+            for i in range(n):
+                x,h=u[0]//2,u[0]%2; b=B2[u[0]%4]; u[0]+=1
+                for cc in range(2): mm2(x,h,cc,b)
+                shade(x,h,b,e)
+                if x==11: store(x,h)
+                elif h: store(x)
+        def s1(j,c,t):
+            for g in range(3): mm1(j,c,t,g,B1[t])
+        def nn(j,c,t): normals(j,c,t,B1[t])
+        s1(1,1,0); s1(1,1,1); nn(1,1,0); quant_b(2,1); nn(1,1,1); quant_b(2,2)
+        s1(1,1,2); s2(2); nn(1,1,2);
+        s1(1,1,3); s2(2); nn(1,1,3); weave_n(1,0,'S'); weave_n(1,1,'V')
+        s1(2,0,0); s2(2); nn(2,0,0); quant_n(1,1)
+        s1(2,0,1); s2(2); nn(2,0,1); quant_n(1,0)
+        s1(2,0,2); s2(1); nn(2,0,2)
+        s1(2,0,3); s2(1); nn(2,0,3); weave_n(2,0,'V')
+        s1(2,1,0); s2(1); nn(2,1,0); quant_n(2,0)
+        s1(2,1,1); s2(1); nn(2,1,1)
+        s1(2,1,2); nn(2,1,2)
+        s1(2,1,3); nn(2,1,3)
+        weave_n(2,1,'V',0); weave_n(2,1,'V',1); quant_n(2,1,0); quant_n(2,1,1)
+        s2(4)
+        for i in range(4): s2(1,'S'); s2(1,'V')

@@ -15,7 +15,17 @@ E4M3 = mybir.dt.float8_e4m3fn_x4
 E2M1 = mybir.dt.float4_e2m1fn_x4
 ALU = mybir.AluOpType
 ACT = mybir.ActivationFunctionType
+
 P = 128
+SLOTS = 4
+SPAN = 512
+BANKS = 8
+CHUNKS = X // SPAN
+GROUPS = C // SPAN
+PASSES = J // SPAN
+ROW_TILES = SPAN // P
+HALVES = R // SPAN
+PER_LANE = X // P
 
 
 def tile_photometric_stereo_shading_s13_kernel(
@@ -23,250 +33,259 @@ def tile_photometric_stereo_shading_s13_kernel(
 ):
     nc = tc.nc
     with ExitStack() as ctx:
-        keep = ctx.enter_context(tc.tile_pool(name="keep", bufs=1))
+        sbuf = ctx.enter_context(tc.tile_pool(name="sbuf", bufs=1))
         psum = ctx.enter_context(tc.psum_pool(name="psum", bufs=1))
         ctx.enter_context(tc.manual_schedule())
 
-        ident = keep.tile([P, P], F32, name="ident")
-        make_identity(nc, ident[:])
-        alb = keep.tile([P, 3, 4], BF16, name="alb")
-        ralb = keep.tile([P, 12], F32, name="ralb")
-        mean = keep.tile([P, 2, 4], BF16, name="mean")
-        w_words = keep.tile([P, 2, 2 * R], U8, name="w_words", align_bytes=64)
-        w_scales = keep.tile([P, 2, R], U8, name="w_scales", align_bytes=64)
-        T = {}
-        banks = {}
+        ident = sbuf.tile([P, P], F32, name="ident")
+        albedo_rows = sbuf.tile([P, PER_LANE], BF16, name="albedo_rows")
+        recip_rows = sbuf.tile([P, PER_LANE], F32, name="recip_rows")
+        recip = sbuf.tile([P, X], F32, name="recip", align_bytes=64)
+        mean_raw = sbuf.tile([P, GROUPS, SLOTS], BF16, name="mean_raw")
+        mean = sbuf.tile([P, GROUPS, SLOTS], F32, name="mean")
+        w_words = sbuf.tile([P, GROUPS, 2 * R], U8, name="w_words", align_bytes=64)
+        w_scales = sbuf.tile([P, GROUPS, R], U8, name="w_scales", align_bytes=64)
 
-        def new(kind, key, shape, dtype, bufs=None):
-            name = "%s_%d_%d" % (kind, key[0], key[1])
-            if bufs is None:
-                T[kind, key] = keep.tile(shape, dtype, name=name, align_bytes=64)
-            else:
-                T[kind, key] = keep.tile(shape, dtype, name=name, tag=kind, bufs=bufs, align_bytes=64)
-            return T[kind, key]
+        raw, woven, codes, scales, shading, bank = {}, {}, {}, {}, {}, {}
+        woven_bufs = {"inv": 3, "img": 4, "nrm": 3}
+        normals_bufs = 4
+        shading_bufs = 2 * ROW_TILES
 
-        def bank(b):
-            banks[b] = psum.tile([P, 512], F32, name="bank%d" % b, tag="bank%d" % b)
-            return banks[b]
+        def label(kind, op):
+            return "%s_%s_%d_%d" % (kind, op[0], op[1], op[2])
 
-        def memset():
-            nc.vector.memset(w_scales[:].rearrange("p g n -> p (g n)").bitcast(I32), 0)
+        def open_bank(b):
+            bank[b] = psum.tile([P, SPAN], F32, name="bank%d" % b, tag="bank%d" % b)
+            return bank[b]
 
-        def load_small(n):
-            if n == "alb":
-                nc.sync.dma_start(out=alb[:], in_=albedo.rearrange("(j p i) -> p j i", p=P, i=4))
-            elif n == "mean":
-                nc.sync.dma_start(out=mean[:], in_=mean_coef.rearrange("(c p t) -> p c t", p=P, t=4))
-            else:
-                for q in range(4):
-                    nc.sync.dma_start(
-                        out=w_scales[32 * q : 32 * q + 4, :, :].bitcast(I32),
-                        in_=lights_scales[:, 4 * q : 4 * q + 4, :].rearrange("g r n -> r g n").bitcast(I32),
-                    )
+        def open_woven(op):
+            if op not in woven:
+                woven[op] = sbuf.tile(
+                    [P, SLOTS * SPAN], BF16, name=label("woven", op), tag="woven_" + op[0],
+                    bufs=woven_bufs[op[0]], align_bytes=64,
+                )
+            return woven[op]
 
-        def load_a(c, g):
-            raw = new("a_raw", (c, g), [P, 4, 512], BF16)
-            src = inverse[512 * c : 512 * (c + 1), 512 * g : 512 * (g + 1)]
-            nc.sync.dma_start(out=raw[:], in_=src.rearrange("(m t) k -> m t k", t=4))
+        def span(i):
+            return slice(SPAN * i, SPAN * (i + 1))
 
-        def load_b(j, g):
-            raw = new("b_raw", (j, g), [P, 4, 512], BF16)
-            src = images[512 * g : 512 * (g + 1), 512 * j : 512 * (j + 1)]
-            nc.sync.dma_start(out=raw[:], in_=src.rearrange("(p t) x -> p t x", t=4))
+        def load_inverse(group, g):
+            op = ("inv", group, g)
+            raw[op] = sbuf.tile([P, SLOTS, SPAN], BF16, name=label("raw", op), align_bytes=64)
+            rows = inverse[span(group), span(g)].rearrange("(m t) k -> m t k", t=SLOTS)
+            nc.sync.dma_start(out=raw[op][:], in_=rows)
 
-        def load_w():
-            nc.sync.dma_start(out=w_words[:].bitcast(I32), in_=lights_words.rearrange("g p b -> p g b").bitcast(I32))
+        def load_images(chunk, g):
+            op = ("img", chunk, g)
+            raw[op] = sbuf.tile([P, SLOTS, SPAN], BF16, name=label("raw", op), align_bytes=64)
+            rows = images[span(g), span(chunk)].rearrange("(p t) x -> p t x", t=SLOTS)
+            nc.sync.dma_start(out=raw[op][:], in_=rows)
 
-        def recip():
-            nc.vector.reciprocal(out=ralb[:], in_=alb[:].rearrange("p j i -> p (j i)"))
+        def load_lights():
+            words = lights_words.rearrange("g p b -> p g b")
+            nc.sync.dma_start(out=w_words[:].bitcast(I32), in_=words.bitcast(I32))
+            for q in range(4):
+                rows = lights_scales[:, 4 * q : 4 * q + 4, :].rearrange("g r n -> r g n")
+                nc.sync.dma_start(out=w_scales[32 * q : 32 * q + 4, :, :].bitcast(I32), in_=rows.bitcast(I32))
 
-        def spread(j, b):
-            acc = bank(b)
+        def spread_recip(b):
+            acc = open_bank(b)
             for i in range(4):
-                col = ralb[:, 4 * j + i : 4 * j + i + 1].to_broadcast([P, P])
-                nc.tensor.transpose(acc[:, P * i : P * (i + 1)], col, ident[:])
-
-        def copy_r(j, b):
-            rinv = new("rinv", (j, 0), [P, 512], F32)
-            nc.scalar.activation(
-                out=rinv[:].rearrange("p (n i) -> p n i", i=4),
-                in_=banks[b][:].rearrange("p (i n) -> p n i", i=4),
-                func=ACT.Copy,
-            )
-
-        def transpose_a(c, g, h, b):
-            acc = bank(b)
-            for t in range(2):
-                words = T["a_raw", (c, g)][:, 2 * h + t, :].bitcast(F32)
-                for u in range(2):
-                    nc.tensor.transpose(acc[:, P * (2 * t + u) : P * (2 * t + u + 1)], words[:, u:256:2], ident[:])
-
-        def copy_a(c, g, h, b):
-            if h == 0:
-                new("a_grp", (c, g), [P, 2048], BF16, bufs=3)
-            dst = T["a_grp", (c, g)][:].bitcast(F32)[:, 512 * h : 512 * (h + 1)]
+                column = recip_rows[:, 4 * b + i : 4 * b + i + 1].to_broadcast([P, P])
+                nc.tensor.transpose(acc[:, P * i : P * (i + 1)], column, ident[:])
             nc.scalar.copy(
-                out=dst.rearrange("p (t m u) -> p t m u", t=2, u=2),
-                in_=banks[b][:].rearrange("p (t u m) -> p t m u", t=2, u=2),
+                out=recip[:].rearrange("p (n b i) -> p b n i", b=PER_LANE // 4, i=4)[:, b, :, :],
+                in_=acc[:].rearrange("p (i n) -> p n i", i=4),
             )
 
-        def quant(kind, key, part):
-            if part != 1:
-                new(kind + "_codes", key, [P, 512], U32)
-                new(kind + "_scales", key, [P, 512], U8)
-            lo, hi = (0, 512) if part == "all" else (256 * part, 256 * part + 256)
+        def turn_inverse(group, g, first_bank):
+            op = ("inv", group, g)
+            for half in range(2):
+                acc = open_bank(first_bank + half)
+                for i in range(2):
+                    words = raw[op][:, 2 * half + i, :].bitcast(F32)
+                    for u in range(2):
+                        at = P * (2 * i + u)
+                        nc.tensor.transpose(acc[:, at : at + P], words[:, u : SPAN // 2 : 2], ident[:])
+            for half in range(2):
+                dst = open_woven(op)[:].bitcast(F32)[:, span(half)]
+                nc.scalar.copy(
+                    out=dst.rearrange("p (i m u) -> p i m u", i=2, u=2),
+                    in_=bank[first_bank + half][:].rearrange("p (i u m) -> p i m u", i=2, u=2),
+                )
+
+        def weave(op, copy, lo=0, hi=SPAN):
+            dst = open_woven(op)[:, SLOTS * lo : SLOTS * hi].rearrange("p (c i t) -> p c t i", i=4, t=SLOTS)
+            copy(out=dst, in_=raw[op][:, :, lo:hi].rearrange("p t (c i) -> p c t i", i=4))
+
+        def weave_shared(op):
+            weave(op, nc.vector.tensor_copy, 0, SPAN // 2)
+            weave(op, nc.scalar.copy, SPAN // 2, SPAN)
+
+        def quantise(op, lo=0, hi=SPAN):
+            if op not in codes:
+                codes[op] = sbuf.tile([P, SPAN], U32, name=label("codes", op), align_bytes=64)
+                scales[op] = sbuf.tile([P, SPAN], U8, name=label("scales", op), align_bytes=64)
             nc.vector.quantize_mx(
-                out=T[kind + "_codes", key][:, lo:hi].bitcast(E4M3),
-                scales=T[kind + "_scales", key][:, lo:hi],
-                in_=T[kind + "_grp", key][:, 4 * lo : 4 * hi],
+                out=codes[op][:, lo:hi].bitcast(E4M3),
+                scales=scales[op][:, lo:hi],
+                in_=woven[op][:, SLOTS * lo : SLOTS * hi],
             )
 
-        def weave(kind, key, e, part, bufs):
-            if part != 1:
-                new(kind + "_grp", key, [P, 2048], BF16, bufs=bufs)
-            lo, hi = (0, 512) if part == "all" else (256 * part, 256 * part + 256)
-            dst = T[kind + "_grp", key][:, 4 * lo : 4 * hi].rearrange("p (c i t) -> p c t i", i=4, t=4)
-            src = T[kind + "_raw", key][:, :, lo:hi].rearrange("p t (c i) -> p c t i", i=4)
-            if e == "V":
-                nc.vector.tensor_copy(out=dst, in_=src)
-            else:
-                nc.scalar.copy(out=dst, in_=src)
-
-        def quant_a(c, g):
-            quant("a", (c, g), "all")
-
-        def quant_b(j, g):
-            quant("b", (j, g), "all")
-
-        def quant_n(j, c, part="all"):
-            quant("n", (j, c), part)
-
-        def weave_b(j, g, e="V", part="all"):
-            weave("b", (j, g), e, part, 4)
-
-        def weave_n(j, c, e="S", part="all"):
-            weave("n", (j, c), e, part, 3)
-
-        def mm1(j, c, t, g, b):
+        def stage1_pass(chunk, group, t, g, b):
             if g == 0:
-                bank(b)
+                open_bank(b)
             cols = slice(P * t, P * (t + 1))
             nc.tensor.matmul_mx(
-                out=banks[b][:],
-                lhsT=T["a_codes", (c, g)][:, cols].bitcast(E4M3),
-                lhsT_scale=T["a_scales", (c, g)][:, cols],
-                rhs=T["b_codes", (j, g)][:].bitcast(E4M3),
-                rhs_scale=T["b_scales", (j, g)][:],
+                out=bank[b][:],
+                lhsT=codes["inv", group, g][:, cols].bitcast(E4M3),
+                lhsT_scale=scales["inv", group, g][:, cols],
+                rhs=codes["img", chunk, g][:].bitcast(E4M3),
+                rhs_scale=scales["img", chunk, g][:],
                 start=(g == 0),
-                stop=(g == 2),
+                stop=(g == PASSES - 1),
             )
 
-        def normals(j, c, t, b):
-            if t == 0:
-                new("n_raw", (j, c), [P, 4, 512], BF16, bufs=4)
-            nc.vector.scalar_tensor_tensor(
-                out=T["n_raw", (j, c)][:, t, :],
-                in0=banks[b][:],
-                scalar=mean[:, c, t : t + 1],
-                in1=T["rinv", (j, 0)][:],
-                op0=ALU.add,
-                op1=ALU.mult,
-            )
+        def stage1_by_pass(group, g):
+            for t in range(SLOTS):
+                stage1_pass(0, group, t, g, t)
 
-        def mm2(x, h, c, b):
-            if c == 0:
-                bank(b)
-            cols = slice(P * (x % 4), P * (x % 4 + 1))
-            nc.tensor.matmul_mx(
-                out=banks[b][:],
-                lhsT=T["n_codes", (x // 4, c)][:, cols].bitcast(E4M3),
-                lhsT_scale=T["n_scales", (x // 4, c)][:, cols],
-                rhs=w_words[:, c, 1024 * h : 1024 * (h + 1)].bitcast(E2M1),
-                rhs_scale=w_scales[:, c, 512 * h : 512 * (h + 1)],
-                start=(c == 0),
-                stop=(c == 1),
-            )
+        def stage1(chunk, group, first_bank):
+            for t in range(SLOTS):
+                for g in range(PASSES):
+                    stage1_pass(chunk, group, t, g, first_bank + t)
 
-        def shade(x, h, b, e="S"):
-            if h == 0:
-                new("shading", (x, 0), [P, R], F32, bufs=8)
-            dst = T["shading", (x, 0)][:, 512 * h : 512 * (h + 1)]
-            if e == "V":
-                nc.vector.tensor_scalar_max(out=dst, in0=banks[b][:], scalar1=0.0)
-            else:
-                nc.scalar.activation(out=dst, in_=banks[b][:], func=ACT.Relu)
+        def normals(chunk, group, first_bank, slots=range(SLOTS)):
+            op = ("nrm", chunk, group)
+            if op not in raw:
+                raw[op] = sbuf.tile(
+                    [P, SLOTS, SPAN], BF16, name=label("raw", op), tag="raw_nrm", bufs=normals_bufs, align_bytes=64
+                )
+            for t in slots:
+                nc.vector.scalar_tensor_tensor(
+                    out=raw[op][:, t, :],
+                    in0=bank[first_bank + t][:],
+                    scalar=mean[:, group, t : t + 1],
+                    in1=recip[:, span(chunk)],
+                    op0=ALU.add,
+                    op1=ALU.mult,
+                )
 
-        def store(x, h="all"):
-            lo, hi = (0, R) if h == "all" else (512 * h, 512 * h + 512)
-            nc.sync.dma_start(out=out[P * x : P * (x + 1), lo:hi], in_=T["shading", (x, 0)][:, lo:hi])
+        def relu_scalar(dst, acc):
+            nc.scalar.activation(out=dst, in_=acc, func=ACT.Relu)
 
+        def relu_vector(dst, acc):
+            nc.vector.tensor_scalar_max(out=dst, in0=acc, scalar1=0.0)
 
-        memset()
-        load_small('alb')
-        for g in range(3): load_a(0,g); load_b(0,g)
-        load_small('mean')
-        load_a(1,0); load_b(1,0); load_a(1,1); load_b(1,1); load_a(1,2); load_b(1,2)
-        load_b(2,0); load_w(); load_small('ws')
-        load_b(2,1); load_b(2,2)
-        recip()
-        def prep_a(s):
-            for h in range(2): transpose_a(s//3,s%3,h,6+h)
-            for h in range(2): copy_a(s//3,s%3,h,6+h)
-        def wb(j,g): weave_b(j,g,'V',0); weave_b(j,g,'S',1)
-        B0=[0,1,2,3]; B1=[4,5,0,1]; B2=[2,3,6,7]
-        spread(0,0); copy_r(0,0); prep_a(0); spread(1,4); spread(2,5)
-        weave_b(0,0,'V')
-        copy_r(1,4)
-        prep_a(1)
-        quant_a(0,0); quant_b(0,0)
-        for t in range(4): mm1(0,0,t,0,B0[t])
-        copy_r(2,5)
-        weave_b(0,1,'V'); quant_a(0,1); quant_b(0,1)
-        prep_a(2)
-        for t in range(4): mm1(0,0,t,1,B0[t])
-        weave_b(0,2,'V'); quant_b(0,2); quant_a(0,2)
-        wb(1,0)
-        prep_a(3)
-        for t in range(4): mm1(0,0,t,2,B0[t])
-        quant_b(1,0); quant_a(1,0);
-        prep_a(4)
-        normals(0,0,0,0); normals(0,0,1,1)
-        for t in range(4): mm1(0,1,t,0,B1[t])
-        wb(1,1); quant_a(1,1); normals(0,0,2,2); quant_b(1,1); normals(0,0,3,3)
-        prep_a(5)
-        for t in range(4): mm1(0,1,t,1,B1[t])
-        quant_a(1,2); wb(1,2);
-        for t in range(4): mm1(0,1,t,2,B1[t])
-        weave_n(0,0,'S'); quant_b(1,2)
-        normals(0,1,0,4); normals(0,1,1,5); normals(0,1,2,0); normals(0,1,3,1)
-        for t in range(4):
-            for g in range(3): mm1(1,0,t,g,B2[t])
-        weave_b(2,0,'S'); quant_n(0,0)
-        weave_n(0,1,'V');
-        normals(1,0,0,2); quant_n(0,1); normals(1,0,1,3); quant_b(2,0); normals(1,0,2,6); normals(1,0,3,7)
-        weave_b(2,1,'S'); wb(2,2)
-        u=[0]
-        def s2(n,e='S'):
-            for i in range(n):
-                x,h=u[0]//2,u[0]%2; b=B2[u[0]%4]; u[0]+=1
-                for cc in range(2): mm2(x,h,cc,b)
-                shade(x,h,b,e)
-                if x==11: store(x,h)
-                elif h: store(x)
-        def s1(j,c,t):
-            for g in range(3): mm1(j,c,t,g,B1[t])
-        def nn(j,c,t): normals(j,c,t,B1[t])
-        s1(1,1,0); s1(1,1,1); nn(1,1,0); quant_b(2,1); nn(1,1,1); quant_b(2,2)
-        s1(1,1,2); s2(2); nn(1,1,2);
-        s1(1,1,3); s2(2); nn(1,1,3); weave_n(1,0,'S'); weave_n(1,1,'V')
-        s1(2,0,0); s2(2); nn(2,0,0); quant_n(1,1)
-        s1(2,0,1); s2(2); nn(2,0,1); quant_n(1,0)
-        s1(2,0,2); s2(1); nn(2,0,2)
-        s1(2,0,3); s2(1); nn(2,0,3); weave_n(2,0,'V')
-        s1(2,1,0); s2(1); nn(2,1,0); quant_n(2,0)
-        s1(2,1,1); s2(1); nn(2,1,1)
-        s1(2,1,2); nn(2,1,2)
-        s1(2,1,3); nn(2,1,3)
-        weave_n(2,1,'V',0); weave_n(2,1,'V',1); quant_n(2,1,0); quant_n(2,1,1)
-        s2(4)
-        for i in range(4): s2(1,'S'); s2(1,'V')
+        def stage2(chunk, first_bank, relus):
+            for i in range(ROW_TILES):
+                rows = slice(SPAN * chunk + P * i, SPAN * chunk + P * (i + 1))
+                cols = slice(P * i, P * (i + 1))
+                last = chunk == CHUNKS - 1 and i == ROW_TILES - 1
+                shading[chunk, i] = sbuf.tile(
+                    [P, R], F32, name="shading_%d_%d" % (chunk, i), tag="shading", bufs=shading_bufs, align_bytes=64
+                )
+                for half in range(HALVES):
+                    acc = open_bank((first_bank + HALVES * i + half) % BANKS)
+                    for group in range(GROUPS):
+                        nc.tensor.matmul_mx(
+                            out=acc[:],
+                            lhsT=codes["nrm", chunk, group][:, cols].bitcast(E4M3),
+                            lhsT_scale=scales["nrm", chunk, group][:, cols],
+                            rhs=w_words[:, group, 2 * SPAN * half : 2 * SPAN * (half + 1)].bitcast(E2M1),
+                            rhs_scale=w_scales[:, group, span(half)],
+                            start=(group == 0),
+                            stop=(group == GROUPS - 1),
+                        )
+                    relus[half](shading[chunk, i][:, span(half)], acc[:])
+                    if last:
+                        nc.sync.dma_start(out=out[rows, span(half)], in_=shading[chunk, i][:, span(half)])
+                if not last:
+                    nc.sync.dma_start(out=out[rows, :], in_=shading[chunk, i][:])
+
+        on_vector, on_scalar = nc.vector.tensor_copy, nc.scalar.copy
+        low, high = 0, BANKS // 2
+
+        make_identity(nc, ident[:])
+        nc.vector.memset(w_scales[:].rearrange("p g n -> p (g n)").bitcast(I32), 0)
+        nc.scalar.dma_start(out=albedo_rows[:], in_=albedo.rearrange("(p i) -> p i", p=P))
+        nc.scalar.dma_start(out=mean_raw[:], in_=mean_coef.rearrange("(c p t) -> p c t", p=P, t=SLOTS))
+        for i in range(GROUPS):
+            for g in range(PASSES):
+                load_inverse(i, g)
+                load_images(i, g)
+        for g in range(PASSES):
+            load_images(2, g)
+        load_lights()
+        nc.vector.reciprocal(out=recip_rows[:], in_=albedo_rows[:])
+        nc.scalar.activation(out=mean[:], in_=mean_raw[:], func=ACT.Copy)
+
+        turn_inverse(0, 0, high)
+        for b in range(PER_LANE // 4):
+            spread_recip(b)
+        turn_inverse(0, 1, high + 2)
+        weave(("img", 0, 0), on_vector)
+        quantise(("inv", 0, 0))
+        quantise(("img", 0, 0))
+        stage1_by_pass(0, 0)
+
+        turn_inverse(0, 2, high)
+        turn_inverse(1, 0, high + 2)
+        weave(("img", 0, 1), on_vector)
+        quantise(("inv", 0, 1))
+        quantise(("img", 0, 1))
+        stage1_by_pass(0, 1)
+        weave(("img", 0, 2), on_vector)
+        quantise(("img", 0, 2))
+        quantise(("inv", 0, 2))
+        stage1_by_pass(0, 2)
+
+        weave_shared(("img", 1, 0))
+        quantise(("inv", 1, 0))
+        quantise(("img", 1, 0))
+        weave_shared(("img", 1, 1))
+        turn_inverse(1, 1, high)
+        turn_inverse(1, 2, high + 2)
+        normals(0, 0, low)
+        stage1_by_pass(1, 0)
+        for g in range(1, PASSES):
+            quantise(("inv", 1, g))
+            stage1_by_pass(1, g)
+        weave_shared(("img", 1, 2))
+        for g in range(1, PASSES):
+            quantise(("img", 1, g))
+
+        weave(("nrm", 0, 0), on_scalar)
+        for g in range(PASSES):
+            weave(("img", 2, g), on_scalar)
+        normals(0, 1, low)
+
+        stage1(1, 0, high)
+        quantise(("nrm", 0, 0))
+        weave(("nrm", 0, 1), on_vector)
+        normals(1, 0, high, [0])
+        quantise(("nrm", 0, 1))
+        normals(1, 0, high, [1, 2, 3])
+        stage1(1, 1, low)
+        normals(1, 1, low)
+        for g in range(PASSES):
+            quantise(("img", 2, g))
+        stage2(0, high, [relu_scalar, relu_scalar])
+
+        weave(("nrm", 1, 0), on_scalar)
+        weave(("nrm", 1, 1), on_vector)
+        stage1(2, 0, high)
+        normals(2, 0, high, [0])
+        quantise(("nrm", 1, 1))
+        normals(2, 0, high, [1, 2, 3])
+        quantise(("nrm", 1, 0))
+        weave(("nrm", 2, 0), on_scalar)
+        stage1(2, 1, low)
+        normals(2, 1, low)
+        quantise(("nrm", 2, 0))
+        for lo in (0, SPAN // 2):
+            weave(("nrm", 2, 1), on_vector, lo, lo + SPAN // 2)
+        for lo in (0, SPAN // 2):
+            quantise(("nrm", 2, 1), lo, lo + SPAN // 2)
+        stage2(1, high, [relu_scalar, relu_scalar])
+        stage2(2, high, [relu_scalar, relu_vector])

from contextlib import ExitStack

import concourse.mybir as mybir
from concourse.masks import make_identity

C, J, X, R = 1024, 1536, 1536, 1024
FLOPS = 2 * C * J * X + 2 * X * C * R

F32 = mybir.dt.float32
BF16 = mybir.dt.bfloat16
I32 = mybir.dt.int32
U32 = mybir.dt.uint32
U8 = mybir.dt.uint8
E4M3 = mybir.dt.float8_e4m3fn_x4
E2M1 = mybir.dt.float4_e2m1fn_x4
ALU = mybir.AluOpType
ACT = mybir.ActivationFunctionType

P = 128
SLOTS = 4
SPAN = 512
BANKS = 8
CHUNKS = X // SPAN
GROUPS = C // SPAN
PASSES = J // SPAN
ROW_TILES = SPAN // P
HALVES = R // SPAN
PER_LANE = X // P


def tile_photometric_stereo_shading_s13_kernel(
    tc, inverse, images, mean_coef, albedo, lights_words, lights_scales, out
):
    nc = tc.nc
    with ExitStack() as ctx:
        sbuf = ctx.enter_context(tc.tile_pool(name="sbuf", bufs=1))
        psum = ctx.enter_context(tc.psum_pool(name="psum", bufs=1))
        ctx.enter_context(tc.manual_schedule())

        ident = sbuf.tile([P, P], F32, name="ident")
        albedo_rows = sbuf.tile([P, PER_LANE], BF16, name="albedo_rows")
        recip_rows = sbuf.tile([P, PER_LANE], F32, name="recip_rows")
        recip = sbuf.tile([P, X], F32, name="recip", align_bytes=64)
        mean_raw = sbuf.tile([P, GROUPS, SLOTS], BF16, name="mean_raw")
        mean = sbuf.tile([P, GROUPS, SLOTS], F32, name="mean")
        w_words = sbuf.tile([P, GROUPS, 2 * R], U8, name="w_words", align_bytes=64)
        w_scales = sbuf.tile([P, GROUPS, R], U8, name="w_scales", align_bytes=64)

        raw, woven, codes, scales, shading, bank = {}, {}, {}, {}, {}, {}
        woven_bufs = {"inv": 3, "img": 4, "nrm": 3}
        normals_bufs = 4
        shading_bufs = 2 * ROW_TILES

        def label(kind, op):
            return "%s_%s_%d_%d" % (kind, op[0], op[1], op[2])

        def open_bank(b):
            bank[b] = psum.tile([P, SPAN], F32, name="bank%d" % b, tag="bank%d" % b)
            return bank[b]

        def open_woven(op):
            if op not in woven:
                woven[op] = sbuf.tile(
                    [P, SLOTS * SPAN], BF16, name=label("woven", op), tag="woven_" + op[0],
                    bufs=woven_bufs[op[0]], align_bytes=64,
                )
            return woven[op]

        def span(i):
            return slice(SPAN * i, SPAN * (i + 1))

        def load_inverse(group, g):
            op = ("inv", group, g)
            raw[op] = sbuf.tile([P, SLOTS, SPAN], BF16, name=label("raw", op), align_bytes=64)
            rows = inverse[span(group), span(g)].rearrange("(m t) k -> m t k", t=SLOTS)
            nc.sync.dma_start(out=raw[op][:], in_=rows)

        def load_images(chunk, g):
            op = ("img", chunk, g)
            raw[op] = sbuf.tile([P, SLOTS, SPAN], BF16, name=label("raw", op), align_bytes=64)
            rows = images[span(g), span(chunk)].rearrange("(p t) x -> p t x", t=SLOTS)
            nc.sync.dma_start(out=raw[op][:], in_=rows)

        def load_lights():
            words = lights_words.rearrange("g p b -> p g b")
            nc.sync.dma_start(out=w_words[:].bitcast(I32), in_=words.bitcast(I32))
            for q in range(4):
                rows = lights_scales[:, 4 * q : 4 * q + 4, :].rearrange("g r n -> r g n")
                nc.sync.dma_start(out=w_scales[32 * q : 32 * q + 4, :, :].bitcast(I32), in_=rows.bitcast(I32))

        def spread_recip(b):
            acc = open_bank(b)
            for i in range(4):
                column = recip_rows[:, 4 * b + i : 4 * b + i + 1].to_broadcast([P, P])
                nc.tensor.transpose(acc[:, P * i : P * (i + 1)], column, ident[:])
            nc.scalar.copy(
                out=recip[:].rearrange("p (n b i) -> p b n i", b=PER_LANE // 4, i=4)[:, b, :, :],
                in_=acc[:].rearrange("p (i n) -> p n i", i=4),
            )

        def turn_inverse(group, g, first_bank):
            op = ("inv", group, g)
            for half in range(2):
                acc = open_bank(first_bank + half)
                for i in range(2):
                    words = raw[op][:, 2 * half + i, :].bitcast(F32)
                    for u in range(2):
                        at = P * (2 * i + u)
                        nc.tensor.transpose(acc[:, at : at + P], words[:, u : SPAN // 2 : 2], ident[:])
            for half in range(2):
                dst = open_woven(op)[:].bitcast(F32)[:, span(half)]
                nc.scalar.copy(
                    out=dst.rearrange("p (i m u) -> p i m u", i=2, u=2),
                    in_=bank[first_bank + half][:].rearrange("p (i u m) -> p i m u", i=2, u=2),
                )

        def weave(op, copy, lo=0, hi=SPAN):
            dst = open_woven(op)[:, SLOTS * lo : SLOTS * hi].rearrange("p (c i t) -> p c t i", i=4, t=SLOTS)
            copy(out=dst, in_=raw[op][:, :, lo:hi].rearrange("p t (c i) -> p c t i", i=4))

        def weave_shared(op):
            weave(op, nc.vector.tensor_copy, 0, SPAN // 2)
            weave(op, nc.scalar.copy, SPAN // 2, SPAN)

        def quantise(op, lo=0, hi=SPAN):
            if op not in codes:
                codes[op] = sbuf.tile([P, SPAN], U32, name=label("codes", op), align_bytes=64)
                scales[op] = sbuf.tile([P, SPAN], U8, name=label("scales", op), align_bytes=64)
            nc.vector.quantize_mx(
                out=codes[op][:, lo:hi].bitcast(E4M3),
                scales=scales[op][:, lo:hi],
                in_=woven[op][:, SLOTS * lo : SLOTS * hi],
            )

        def stage1_pass(chunk, group, t, g, b):
            if g == 0:
                open_bank(b)
            cols = slice(P * t, P * (t + 1))
            nc.tensor.matmul_mx(
                out=bank[b][:],
                lhsT=codes["inv", group, g][:, cols].bitcast(E4M3),
                lhsT_scale=scales["inv", group, g][:, cols],
                rhs=codes["img", chunk, g][:].bitcast(E4M3),
                rhs_scale=scales["img", chunk, g][:],
                start=(g == 0),
                stop=(g == PASSES - 1),
            )

        def stage1_by_pass(group, g):
            for t in range(SLOTS):
                stage1_pass(0, group, t, g, t)

        def stage1(chunk, group, first_bank):
            for t in range(SLOTS):
                for g in range(PASSES):
                    stage1_pass(chunk, group, t, g, first_bank + t)

        def normals(chunk, group, first_bank, slots=range(SLOTS)):
            op = ("nrm", chunk, group)
            if op not in raw:
                raw[op] = sbuf.tile(
                    [P, SLOTS, SPAN], BF16, name=label("raw", op), tag="raw_nrm", bufs=normals_bufs, align_bytes=64
                )
            for t in slots:
                nc.vector.scalar_tensor_tensor(
                    out=raw[op][:, t, :],
                    in0=bank[first_bank + t][:],
                    scalar=mean[:, group, t : t + 1],
                    in1=recip[:, span(chunk)],
                    op0=ALU.add,
                    op1=ALU.mult,
                )

        def relu_scalar(dst, acc):
            nc.scalar.activation(out=dst, in_=acc, func=ACT.Relu)

        def relu_vector(dst, acc):
            nc.vector.tensor_scalar_max(out=dst, in0=acc, scalar1=0.0)

        def stage2(chunk, first_bank, relus):
            for i in range(ROW_TILES):
                rows = slice(SPAN * chunk + P * i, SPAN * chunk + P * (i + 1))
                cols = slice(P * i, P * (i + 1))
                last = chunk == CHUNKS - 1 and i == ROW_TILES - 1
                shading[chunk, i] = sbuf.tile(
                    [P, R], F32, name="shading_%d_%d" % (chunk, i), tag="shading", bufs=shading_bufs, align_bytes=64
                )
                for half in range(HALVES):
                    acc = open_bank((first_bank + HALVES * i + half) % BANKS)
                    for group in range(GROUPS):
                        nc.tensor.matmul_mx(
                            out=acc[:],
                            lhsT=codes["nrm", chunk, group][:, cols].bitcast(E4M3),
                            lhsT_scale=scales["nrm", chunk, group][:, cols],
                            rhs=w_words[:, group, 2 * SPAN * half : 2 * SPAN * (half + 1)].bitcast(E2M1),
                            rhs_scale=w_scales[:, group, span(half)],
                            start=(group == 0),
                            stop=(group == GROUPS - 1),
                        )
                    relus[half](shading[chunk, i][:, span(half)], acc[:])
                    if last:
                        nc.sync.dma_start(out=out[rows, span(half)], in_=shading[chunk, i][:, span(half)])
                if not last:
                    nc.sync.dma_start(out=out[rows, :], in_=shading[chunk, i][:])

        on_vector, on_scalar = nc.vector.tensor_copy, nc.scalar.copy
        low, high = 0, BANKS // 2

        make_identity(nc, ident[:])
        nc.vector.memset(w_scales[:].rearrange("p g n -> p (g n)").bitcast(I32), 0)
        nc.scalar.dma_start(out=albedo_rows[:], in_=albedo.rearrange("(p i) -> p i", p=P))
        nc.scalar.dma_start(out=mean_raw[:], in_=mean_coef.rearrange("(c p t) -> p c t", p=P, t=SLOTS))
        for i in range(GROUPS):
            for g in range(PASSES):
                load_inverse(i, g)
                load_images(i, g)
        for g in range(PASSES):
            load_images(2, g)
        load_lights()
        nc.vector.reciprocal(out=recip_rows[:], in_=albedo_rows[:])
        nc.scalar.activation(out=mean[:], in_=mean_raw[:], func=ACT.Copy)

        turn_inverse(0, 0, high)
        for b in range(PER_LANE // 4):
            spread_recip(b)
        turn_inverse(0, 1, high + 2)
        weave(("img", 0, 0), on_vector)
        quantise(("inv", 0, 0))
        quantise(("img", 0, 0))
        stage1_by_pass(0, 0)

        turn_inverse(0, 2, high)
        turn_inverse(1, 0, high + 2)
        weave(("img", 0, 1), on_vector)
        quantise(("inv", 0, 1))
        quantise(("img", 0, 1))
        stage1_by_pass(0, 1)
        weave(("img", 0, 2), on_vector)
        quantise(("img", 0, 2))
        quantise(("inv", 0, 2))
        stage1_by_pass(0, 2)

        weave_shared(("img", 1, 0))
        quantise(("inv", 1, 0))
        quantise(("img", 1, 0))
        weave_shared(("img", 1, 1))
        turn_inverse(1, 1, high)
        turn_inverse(1, 2, high + 2)
        normals(0, 0, low)
        stage1_by_pass(1, 0)
        for g in range(1, PASSES):
            quantise(("inv", 1, g))
            stage1_by_pass(1, g)
        weave_shared(("img", 1, 2))
        for g in range(1, PASSES):
            quantise(("img", 1, g))

        weave(("nrm", 0, 0), on_scalar)
        for g in range(PASSES):
            weave(("img", 2, g), on_scalar)
        normals(0, 1, low)

        stage1(1, 0, high)
        quantise(("nrm", 0, 0))
        weave(("nrm", 0, 1), on_vector)
        normals(1, 0, high, [0])
        quantise(("nrm", 0, 1))
        normals(1, 0, high, [1, 2, 3])
        stage1(1, 1, low)
        normals(1, 1, low)
        for g in range(PASSES):
            quantise(("img", 2, g))
        stage2(0, high, [relu_scalar, relu_scalar])

        weave(("nrm", 1, 0), on_scalar)
        weave(("nrm", 1, 1), on_vector)
        stage1(2, 0, high)
        normals(2, 0, high, [0])
        quantise(("nrm", 1, 1))
        normals(2, 0, high, [1, 2, 3])
        quantise(("nrm", 1, 0))
        weave(("nrm", 2, 0), on_scalar)
        stage1(2, 1, low)
        normals(2, 1, low)
        quantise(("nrm", 2, 0))
        for lo in (0, SPAN // 2):
            weave(("nrm", 2, 1), on_vector, lo, lo + SPAN // 2)
        for lo in (0, SPAN // 2):
            quantise(("nrm", 2, 1), lo, lo + SPAN // 2)
        stage2(1, high, [relu_scalar, relu_scalar])
        stage2(2, high, [relu_scalar, relu_vector])
